import numpy as np
import ml_dtypes


def mxq(x, axis, fmt="e4m3"):
    dtype, down = {"e4m3": (ml_dtypes.float8_e4m3fn, 7), "e5m2": (ml_dtypes.float8_e5m2, 14)}[fmt]
    v = np.moveaxis(np.asarray(x, np.float32).astype(ml_dtypes.bfloat16).astype(np.float64), axis, -1)
    blocks = v.reshape(v.shape[:-1] + (-1, 32))
    amax = np.abs(blocks).max(-1, keepdims=True)
    byte = np.maximum(np.where(amax > 0, np.frexp(amax)[1] - 1 + 127, 0) - down, 1)
    scale = np.exp2(byte - 127.0)
    codes = (blocks / scale).astype(np.float32).astype(dtype).astype(np.float64)
    return np.moveaxis((codes * scale).reshape(v.shape), -1, axis)


WIDE = False


def mx_kscale(k):
    if not WIDE:
        return np.ones(k)
    levels = np.array([30, -30])
    if k % 512:
        return np.exp2(np.random.permutation(np.resize(levels, k // 32))).repeat(32)
    a = np.empty((k // 512, 16))
    for p in range(k // 512):
        a[p, :8] = np.random.permutation(np.resize(levels, 8))
        for g in range(8):
            far = levels[np.abs(levels - a[p, g]) >= 10]
            a[p, g + 8] = far[np.random.randint(len(far))]
    return np.exp2(a.ravel()).repeat(32)


def f64(x):
    return np.asarray(x).astype(np.float64)


def striped(idx):
    return np.tile(np.asarray(idx).reshape(-1, 16).T, (8, 1)).astype(np.uint16)


def unstriped(offs):
    return offs[:16].T.reshape(-1).astype(np.int64)


E2M1 = np.array([0.0, 0.5, 1.0, 1.5, 2.0, 3.0, 4.0, 6.0, -0.0, -0.5, -1.0, -1.5, -2.0, -3.0, -4.0, -6.0])


def pack_weight(w, fmt):
    k, n = w.shape
    w = f64(np.asarray(w, np.float32).astype(ml_dtypes.bfloat16)).reshape(k // 32, 32, n)
    amax = np.abs(w).max(1)
    if fmt in ("e4m3", "e5m2"):
        byte = np.frexp(amax)[1] - 1 + 127 - (7 if fmt == "e4m3" else 14)
    else:
        mant, ex = np.frexp(amax / 6.0)
        byte = np.where(mant > 0.5, ex, ex - 1) + 127
    byte = np.clip(np.where(amax > 0, byte, 1), 1, 254)
    scaled = (w * np.exp2(127.0 - byte)[:, None, :]).reshape(k, n).astype(np.float32)
    by_word = np.ascontiguousarray(scaled.reshape(k // 512, 128, 4, n).transpose(0, 1, 3, 2))
    if fmt in ("e4m3", "e5m2"):
        words = by_word.astype(ml_dtypes.float8_e4m3fn if fmt == "e4m3" else ml_dtypes.float8_e5m2).view(np.uint8)
    else:
        c = by_word.astype(ml_dtypes.float4_e2m1fn).view(np.uint8) & 0xF
        words = (c[..., 0::2] | (c[..., 1::2] << 4)).reshape(k // 512, 128, 2 * n)
    return np.ascontiguousarray(words), np.ascontiguousarray(byte.astype(np.uint8).reshape(k // 512, 16, n))


def unpack_weight(words, scales, fmt):
    g, _, n = scales.shape
    words = np.ascontiguousarray(words).reshape(g, 128, n, -1)
    if fmt in ("e4m3", "e5m2"):
        vals = words.view(ml_dtypes.float8_e4m3fn if fmt == "e4m3" else ml_dtypes.float8_e5m2).astype(np.float64)
    else:
        nib = np.empty((g, 128, n, 4), np.uint8)
        nib[..., 0::2] = words & 0xF
        nib[..., 1::2] = words >> 4
        vals = E2M1[nib]
    vals = vals * np.repeat(np.exp2(scales.astype(np.float64) - 127.0), 8, axis=1)[..., None]
    return vals.transpose(0, 1, 3, 2).reshape(g * 512, n)


K, T, J, I, S, V = 1024, 1024, 256, 256, 512, 1024


def setup_inputs():
    n = np.random.standard_normal
    idx = np.random.permutation(T)[:J]
    idx2 = np.random.permutation(S)[:J]
    idx3 = np.random.permutation(V)[:I]
    fk = mx_kscale(K)
    kyp = pack_weight(n((K, V)) / fk[:, None], "e5m2")
    return {
        "xf": (n((K, T)) * 0.03).astype(np.float32),
        "xb": (n((K, S))).astype(np.float32),
        "fk": (np.random.uniform(0.5, 2.0, (K, 1)) * fk[:, None]).astype(np.float32),
        "ky_words": kyp[0],
        "ky_scales": kyp[1],
        "bi": (np.random.uniform(-0.7, 0.7, (1, I))).astype(np.float32),
        "tg": (np.random.uniform(-0.5, 1.5, (J, 1))).astype(np.float32),
        "offs": striped(idx),
        "offs2": striped(idx2),
        "offs3": striped(idx3),
    }


def reference(xf, xb, fk, ky_words, ky_scales, bi, tg, offs, offs2, offs3):
    idx = unstriped(offs)
    idx2 = unstriped(offs2)
    idx3 = unstriped(offs3)
    kyu = unpack_weight(ky_words, ky_scales, "e5m2")
    u = f64(xf)[:, idx] * f64(xb)[:, idx2] * f64(fk)
    uq = mxq(u, 0, "e5m2")
    kyidx3g = kyu[:, idx3]
    a0 = uq.T @ kyidx3g
    a = a0 + f64(bi)
    y = np.square(np.maximum(a - f64(tg), 0.0))
    return y

@@ -1,0 +1,185 @@
+from contextlib import ExitStack
+
+import concourse.mybir as mybir
+from concourse.masks import make_identity
+
+K, T, J, I, S, V = 1024, 1024, 256, 256, 512, 1024
+FLOPS = 2 * K * J * I
+
+F32 = mybir.dt.float32
+BF16 = mybir.dt.bfloat16
+I32 = mybir.dt.int32
+U32 = mybir.dt.uint32
+U16 = mybir.dt.uint16
+U8 = mybir.dt.uint8
+E5M2X4 = mybir.dt.float8_e5m2_x4
+ALU = mybir.AluOpType
+ACT = mybir.ActivationFunctionType
+
+P = 128
+PACK = 4
+PASSES = K // (P * PACK)
+HALF = 128
+LIST_COLS = HALF // 16
+
+
+def tile_list_scores_products_listed_hinge_kernel(tc, xf, xb, fk, ky_words, ky_scales, bi, tg, offs, offs2, offs3, out):
+    nc = tc.nc
+    with ExitStack() as ctx:
+        keep = ctx.enter_context(tc.tile_pool(name="keep", bufs=1))
+        psum = ctx.enter_context(tc.psum_pool(name="psum", bufs=1))
+
+        planes = PASSES * PACK
+        tok_list = keep.tile([P, J // 16], U16, name="tok_list")
+        ent_list = keep.tile([P, J // 16], U16, name="ent_list")
+        key_list = keep.tile([P, I // 16], U16, name="key_list")
+        xf_planes = [keep.tile([P, T], F32, name=f"xf{g}") for g in range(planes)]
+        xb_pairs = [keep.tile([P, 2 * S], F32, name=f"xb{u}") for u in range(planes // 2)]
+        words = [keep.tile([P, V], I32, name=f"words{z}") for z in range(PASSES)]
+        key_scales = keep.tile([P, PASSES * V], U8, name="key_scales")
+        factors = keep.tile([P, PASSES, PACK], F32, name="factors")
+        bias_cols = keep.tile([P, 2], F32, name="bias_cols")
+        targets = keep.tile([P, 2], F32, name="targets")
+        ident = keep.tile([P, P], F32, name="ident")
+
+        xf_view = xf.rearrange("(z p t) c -> z t p c", z=PASSES, t=PACK)
+        xb_view = xb.rearrange("(z p u e) c -> z u p (e c)", z=PASSES, u=2, e=2)
+        scale_rows = ky_scales.bitcast(I32)
+
+        def load_xf(g):
+            nc.sync.dma_start(out=xf_planes[g][:], in_=xf_view[g // PACK, g % PACK])
+
+        def load_xb(u):
+            nc.sync.dma_start(out=xb_pairs[u][:], in_=xb_view[u // 2, u % 2])
+
+        def load_words(z):
+            nc.sync.dma_start(out=words[z][:], in_=ky_words[z].rearrange("p c r -> p (c r)").bitcast(I32))
+
+        def load_scales(q):
+            nc.sync.dma_start(
+                out=key_scales[32 * q : 32 * q + 4, :].bitcast(I32).rearrange("p (z c) -> p z c", z=PASSES),
+                in_=scale_rows[:, 4 * q : 4 * q + 4, :].rearrange("z r c -> r z c"),
+            )
+
+        nc.vector.memset(key_scales[:].bitcast(I32), 0)
+        make_identity(nc, ident[:])
+        load_xb(0)
+        nc.sync.dma_start(ent_list[:], offs2)
+        nc.sync.dma_start(out=factors[:], in_=fk.rearrange("(z p t) o -> p z (t o)", z=PASSES, t=PACK))
+        nc.sync.dma_start(tok_list[:], offs)
+        load_xf(0)
+        load_xf(1)
+        load_xb(1)
+        nc.sync.dma_start(key_list[:], offs3)
+        load_scales(0)
+        load_scales(1)
+        load_xf(2)
+        load_scales(2)
+        load_scales(3)
+        load_xf(3)
+        load_xb(2)
+        with nc.allow_non_contiguous_dma(reason="one value a partition"):
+            nc.sync.dma_start(out=bias_cols[:], in_=bi.rearrange("o (h n) -> n (o h)", h=2))
+            load_xf(4)
+            nc.sync.dma_start(out=targets[:], in_=tg.rearrange("(h n) o -> n (h o)", h=2))
+        load_xb(3)
+        for g in range(5, planes):
+            load_xf(g)
+        for z in range(PASSES):
+            load_words(z)
+
+        prod = [keep.tile([P, PACK, J], F32, name=f"prod{z}") for z in range(PASSES)]
+        u_codes = [keep.tile([P, J], U32, name=f"u_codes{z}", align_bytes=64) for z in range(PASSES)]
+        u_scales = [keep.tile([P, J], U8, name=f"u_scales{z}", align_bytes=64) for z in range(PASSES)]
+        picked_scales = [keep.tile([P, I], U8, name=f"picked_scales{z}", align_bytes=64) for z in range(PASSES)]
+        less = keep.tile([P, 2, 2, HALF], F32, name="less")
+
+        def product(g):
+            z, t = divmod(g, PACK)
+            picked = keep.tile([P, J], F32, name=f"picked{g}")
+            window = xb_pairs[g // 2][:, (g % 2) * S : (g % 2 + 1) * S]
+            nc.scalar.activation(picked[:], window.indirect(ent_list[:]), ACT.Copy)
+            scaled = keep.tile([P, J], F32, name=f"scaled{g}")
+            nc.scalar.activation(scaled[:], picked[:], ACT.Copy, scale=factors[:, z, t : t + 1])
+            pieces = 2 if g == planes - 1 else 1
+            width = J // pieces
+            for m in range(pieces):
+                cols = slice(m * width, (m + 1) * width)
+                nc.vector.tensor_tensor(
+                    prod[z][:, t, cols],
+                    xf_planes[g][:].indirect(tok_list[:, m * width // 16 : (m + 1) * width // 16]),
+                    scaled[:, cols],
+                    ALU.mult,
+                )
+
+        def quantize(z):
+            woven = keep.tile([P, J * PACK], BF16, name=f"woven{z}", align_bytes=64)
+            for m in range(2):
+                dst = woven[:, m * HALF * PACK : (m + 1) * HALF * PACK].rearrange("p (c i t) -> p c t i", i=4, t=PACK)
+                src = prod[z][:, :, m * HALF : (m + 1) * HALF].rearrange("p t (c i) -> p c t i", i=4)
+                if m == 0:
+                    nc.scalar.copy(dst, src)
+                else:
+                    nc.vector.tensor_copy(dst, src)
+            nc.vector.quantize_mx(out=u_codes[z][:].bitcast(E5M2X4), scales=u_scales[z][:], in_=woven[:])
+
+        def pick_scales(z):
+            nc.vector.tensor_copy(picked_scales[z][:], key_scales[:, z * V : (z + 1) * V].indirect(key_list[:]))
+
+        def thresholds():
+            bias_rows = psum.tile([P, 2, HALF], F32, name="bias_rows")
+            for h in range(2):
+                nc.tensor.transpose(bias_rows[:, h, :], bias_cols[:, h : h + 1].to_broadcast([P, P]), ident[:])
+            for m in range(2):
+                nc.scalar.activation(
+                    less[:, :, m, :], bias_rows[:], ACT.Identity, bias=targets[:, m : m + 1], scale=-1.0
+                )
+
+        for g in range(PACK):
+            product(g)
+        pick_scales(0)
+        quantize(0)
+        product(PACK)
+        pick_scales(1)
+        for g in range(PACK + 1, planes):
+            product(g)
+        thresholds()
+        quantize(1)
+
+        picked_words = {}
+        for z in range(PASSES):
+            for h in range(2):
+                picked_words[z, h] = keep.tile([P, HALF], U32, name=f"picked_words{z}_{h}", align_bytes=64)
+                nc.vector.tensor_copy(
+                    picked_words[z, h][:],
+                    words[z][:].bitcast(U32).indirect(key_list[:, h * LIST_COLS : (h + 1) * LIST_COLS]),
+                )
+
+        sums = [psum.tile([P, 2, HALF], F32, name=f"sums{h}") for h in range(2)]
+        for z in range(PASSES):
+            for h in range(2):
+                for m in range(2):
+                    nc.tensor.matmul_mx(
+                        out=sums[h][:, m, :],
+                        lhsT=u_codes[z][:, m * HALF : (m + 1) * HALF].bitcast(E5M2X4),
+                        lhsT_scale=u_scales[z][:, m * HALF : (m + 1) * HALF],
+                        rhs=picked_words[z, h][:].bitcast(E5M2X4),
+                        rhs_scale=picked_scales[z][:, h * HALF : (h + 1) * HALF],
+                        start=(z == 0 and m == 0),
+                        stop=(z == PASSES - 1 and m == 1),
+                    )
+
+        out_view = out.rearrange("(m p) (h n) -> h p m n", m=2, h=2)
+        margin = [keep.tile([P, 2 * HALF], F32, name=f"margin{h}") for h in range(2)]
+        for h in range(2):
+            nc.vector.tensor_tensor(
+                margin[h][:],
+                sums[h][:].rearrange("p m n -> p (m n)"),
+                less[:, h].rearrange("p m n -> p (m n)"),
+                ALU.subtract,
+            )
+        for h in range(2):
+            result = keep.tile([P, 2 * HALF], F32, name=f"result{h}")
+            nc.vector.scalar_tensor_tensor(result[:], margin[h][:], 0.0, margin[h][:], ALU.max, ALU.mult)
+            queue = nc.sync if h == 0 else nc.scalar
+            queue.dma_start(out=out_view[h], in_=result[:].rearrange("p (m n) -> p m n", m=2))

@@ -1,7 +1,6 @@
 from contextlib import ExitStack
 
 import concourse.mybir as mybir
-from concourse.masks import make_identity
 
 K, T, J, I, S, V = 1024, 1024, 256, 256, 512, 1024
 FLOPS = 2 * K * J * I
@@ -62,7 +61,13 @@ def tile_list_scores_products_listed_hinge_kernel(tc, xf, xb, fk, ky_words, ky_s
             )
 
         nc.vector.memset(key_scales[:].bitcast(I32), 0)
-        make_identity(nc, ident[:])
+        distance = keep.tile([P, P], F32, name="distance", tag="picked1")
+        nc.gpsimd.iota(
+            distance[:], pattern=[[1, P]], base=0, channel_multiplier=-1, allow_small_or_imprecise_dtypes=True
+        )
+        magnitude = keep.tile([P, P], F32, name="magnitude", tag="picked0")
+        nc.scalar.activation(magnitude[:], distance[:], ACT.Abs)
+        nc.scalar.activation(ident[:], magnitude[:], ACT.Relu, bias=1.0, scale=-1.0)
         load_xb(0)
         nc.sync.dma_start(ent_list[:], offs2)
         nc.sync.dma_start(out=factors[:], in_=fk.rearrange("(z p t) o -> p z (t o)", z=PASSES, t=PACK))
@@ -71,18 +76,18 @@ def tile_list_scores_products_listed_hinge_kernel(tc, xf, xb, fk, ky_words, ky_s
         load_xf(1)
         load_xb(1)
         nc.sync.dma_start(key_list[:], offs3)
-        load_scales(0)
-        load_scales(1)
         load_xf(2)
-        load_scales(2)
-        load_scales(3)
+        load_scales(0)
         load_xf(3)
+        load_scales(1)
+        load_scales(2)
         load_xb(2)
+        load_scales(3)
+        load_xb(3)
         with nc.allow_non_contiguous_dma(reason="one value a partition"):
             nc.sync.dma_start(out=bias_cols[:], in_=bi.rearrange("o (h n) -> n (o h)", h=2))
             load_xf(4)
             nc.sync.dma_start(out=targets[:], in_=tg.rearrange("(h n) o -> n (h o)", h=2))
-        load_xb(3)
         for g in range(5, planes):
             load_xf(g)
         for z in range(PASSES):
@@ -92,11 +97,12 @@ def tile_list_scores_products_listed_hinge_kernel(tc, xf, xb, fk, ky_words, ky_s
         u_codes = [keep.tile([P, J], U32, name=f"u_codes{z}", align_bytes=64) for z in range(PASSES)]
         u_scales = [keep.tile([P, J], U8, name=f"u_scales{z}", align_bytes=64) for z in range(PASSES)]
         picked_scales = [keep.tile([P, I], U8, name=f"picked_scales{z}", align_bytes=64) for z in range(PASSES)]
+        wovens = [keep.tile([P, J * PACK], BF16, name=f"woven{z}", align_bytes=64) for z in range(PASSES)]
         less = keep.tile([P, 2, 2, HALF], F32, name="less")
 
         def product(g):
             z, t = divmod(g, PACK)
-            picked = keep.tile([P, J], F32, name=f"picked{g}")
+            picked = keep.tile([P, J], F32, name=f"picked{g}", tag=f"picked{g}")
             window = xb_pairs[g // 2][:, (g % 2) * S : (g % 2 + 1) * S]
             nc.scalar.activation(picked[:], window.indirect(ent_list[:]), ACT.Copy)
             scaled = keep.tile([P, J], F32, name=f"scaled{g}")
@@ -112,16 +118,27 @@ def tile_list_scores_products_listed_hinge_kernel(tc, xf, xb, fk, ky_words, ky_s
                     ALU.mult,
                 )
 
+        def weave(z):
+            woven = wovens[z]
+            copies = [nc.scalar.copy, nc.vector.tensor_copy] if z == PASSES - 1 else [nc.vector.tensor_copy]
+            width = J // len(copies)
+            for m, copy in enumerate(copies):
+                dst = woven[:, m * width * PACK : (m + 1) * width * PACK].rearrange("p (c i t) -> p c t i", i=4, t=PACK)
+                src = prod[z][:, :, m * width : (m + 1) * width].rearrange("p t (c i) -> p c t i", i=4)
+                copy(dst, src)
+
         def quantize(z):
-            woven = keep.tile([P, J * PACK], BF16, name=f"woven{z}", align_bytes=64)
-            for m in range(2):
-                dst = woven[:, m * HALF * PACK : (m + 1) * HALF * PACK].rearrange("p (c i t) -> p c t i", i=4, t=PACK)
-                src = prod[z][:, :, m * HALF : (m + 1) * HALF].rearrange("p t (c i) -> p c t i", i=4)
-                if m == 0:
-                    nc.scalar.copy(dst, src)
-                else:
-                    nc.vector.tensor_copy(dst, src)
-            nc.vector.quantize_mx(out=u_codes[z][:].bitcast(E5M2X4), scales=u_scales[z][:], in_=woven[:])
+            nc.vector.quantize_mx(out=u_codes[z][:].bitcast(E5M2X4), scales=u_scales[z][:], in_=wovens[z][:])
+
+        picked_words = {}
+
+        def pick_words(z):
+            for h in range(2):
+                picked_words[z, h] = keep.tile([P, HALF], U32, name=f"picked_words{z}_{h}", align_bytes=64)
+                nc.vector.tensor_copy(
+                    picked_words[z, h][:],
+                    words[z][:].bitcast(U32).indirect(key_list[:, h * LIST_COLS : (h + 1) * LIST_COLS]),
+                )
 
         def pick_scales(z):
             nc.vector.tensor_copy(picked_scales[z][:], key_scales[:, z * V : (z + 1) * V].indirect(key_list[:]))
@@ -137,23 +154,17 @@ def tile_list_scores_products_listed_hinge_kernel(tc, xf, xb, fk, ky_words, ky_s
 
         for g in range(PACK):
             product(g)
+        weave(0)
         pick_scales(0)
         quantize(0)
-        product(PACK)
         pick_scales(1)
-        for g in range(PACK + 1, planes):
+        for g in range(PACK, planes):
             product(g)
         thresholds()
+        weave(1)
+        pick_words(0)
         quantize(1)
-
-        picked_words = {}
-        for z in range(PASSES):
-            for h in range(2):
-                picked_words[z, h] = keep.tile([P, HALF], U32, name=f"picked_words{z}_{h}", align_bytes=64)
-                nc.vector.tensor_copy(
-                    picked_words[z, h][:],
-                    words[z][:].bitcast(U32).indirect(key_list[:, h * LIST_COLS : (h + 1) * LIST_COLS]),
-                )
+        pick_words(1)
 
         sums = [psum.tile([P, 2, HALF], F32, name=f"sums{h}") for h in range(2)]
         for z in range(PASSES):
@@ -180,6 +191,11 @@ def tile_list_scores_products_listed_hinge_kernel(tc, xf, xb, fk, ky_words, ky_s
             )
         for h in range(2):
             result = keep.tile([P, 2 * HALF], F32, name=f"result{h}")
-            nc.vector.scalar_tensor_tensor(result[:], margin[h][:], 0.0, margin[h][:], ALU.max, ALU.mult)
-            queue = nc.sync if h == 0 else nc.scalar
+            if h == 0:
+                excess = keep.tile([P, 2 * HALF], F32, name="excess")
+                nc.scalar.activation(excess[:], margin[h][:], ACT.Relu)
+                nc.scalar.activation(result[:], excess[:], ACT.Square)
+            else:
+                nc.vector.scalar_tensor_tensor(result[:], margin[h][:], 0.0, margin[h][:], ALU.max, ALU.mult)
+            queue = nc.scalar if h == 0 else nc.sync
             queue.dma_start(out=out_view[h], in_=result[:].rearrange("p (m n) -> p m n", m=2))

@@ -34,11 +34,12 @@ def tile_list_scores_products_listed_hinge_kernel(tc, xf, xb, fk, ky_words, ky_s
         key_list = keep.tile([P, I // 16], U16, name="key_list")
         xf_planes = [keep.tile([P, T], F32, name=f"xf{g}") for g in range(planes)]
         xb_pairs = [keep.tile([P, 2 * S], F32, name=f"xb{u}") for u in range(planes // 2)]
-        words = [keep.tile([P, V], I32, name=f"words{z}") for z in range(PASSES)]
+        words = [keep.tile([P, V], I32, name=f"words{z}", tag=f"words{z}", align_bytes=64) for z in range(PASSES)]
         key_scales = keep.tile([P, PASSES * V], U8, name="key_scales")
-        factors = keep.tile([P, PASSES, PACK], F32, name="factors")
-        bias_cols = keep.tile([P, 2], F32, name="bias_cols")
-        targets = keep.tile([P, 2], F32, name="targets")
+        rows = keep.tile([P, P * PACK], F32, name="rows")
+        factors = keep.tile([P, PACK, PASSES], F32, name="factors")
+        columns = keep.tile([P, 4], F32, name="columns")
+        shift = keep.tile([P, 2, 2, HALF], F32, name="shift")
         ident = keep.tile([P, P], F32, name="ident")
 
         xf_view = xf.rearrange("(z p t) c -> z t p c", z=PASSES, t=PACK)
@@ -60,59 +61,59 @@ def tile_list_scores_products_listed_hinge_kernel(tc, xf, xb, fk, ky_words, ky_s
                 in_=scale_rows[:, 4 * q : 4 * q + 4, :].rearrange("z r c -> r z c"),
             )
 
+        nc.vector.memset(rows[:], 0.0)
         nc.vector.memset(key_scales[:].bitcast(I32), 0)
-        distance = keep.tile([P, P], F32, name="distance", tag="picked1")
+        distance = keep.tile([P, P], F32, name="distance", tag="picked0")
         nc.gpsimd.iota(
             distance[:], pattern=[[1, P]], base=0, channel_multiplier=-1, allow_small_or_imprecise_dtypes=True
         )
-        magnitude = keep.tile([P, P], F32, name="magnitude", tag="picked0")
+        magnitude = keep.tile([P, P], F32, name="magnitude", tag="picked1")
         nc.scalar.activation(magnitude[:], distance[:], ACT.Abs)
         nc.scalar.activation(ident[:], magnitude[:], ACT.Relu, bias=1.0, scale=-1.0)
         load_xb(0)
+        nc.sync.dma_start(out=rows[0:2, :], in_=fk.rearrange("(z k) o -> z (k o)", z=PASSES))
+        nc.sync.dma_start(out=rows[2:4, 0:HALF], in_=tg.rearrange("(m p) o -> m (p o)", m=2))
+        nc.sync.dma_start(out=rows[4:6, 0:HALF], in_=bi.rearrange("o (h n) -> (o h) n", h=2))
         nc.sync.dma_start(ent_list[:], offs2)
-        nc.sync.dma_start(out=factors[:], in_=fk.rearrange("(z p t) o -> p z (t o)", z=PASSES, t=PACK))
         nc.sync.dma_start(tok_list[:], offs)
         load_xf(0)
-        load_xf(1)
         load_xb(1)
         nc.sync.dma_start(key_list[:], offs3)
-        load_xf(2)
+        load_xf(1)
         load_scales(0)
-        load_xf(3)
+        load_xb(2)
         load_scales(1)
         load_scales(2)
-        load_xb(2)
+        load_xf(2)
         load_scales(3)
         load_xb(3)
-        with nc.allow_non_contiguous_dma(reason="one value a partition"):
-            nc.sync.dma_start(out=bias_cols[:], in_=bi.rearrange("o (h n) -> n (o h)", h=2))
-            load_xf(4)
-            nc.sync.dma_start(out=targets[:], in_=tg.rearrange("(h n) o -> n (h o)", h=2))
-        for g in range(5, planes):
+        load_xf(3)
+        for g in range(4, planes):
             load_xf(g)
         for z in range(PASSES):
             load_words(z)
 
-        prod = [keep.tile([P, PACK, J], F32, name=f"prod{z}") for z in range(PASSES)]
-        u_codes = [keep.tile([P, J], U32, name=f"u_codes{z}", align_bytes=64) for z in range(PASSES)]
+        pieces_of = [1, 2]
+        prod = [
+            [keep.tile([P, PACK, J // pieces_of[z]], F32, name=f"prod{z}_{m}") for m in range(pieces_of[z])]
+            for z in range(PASSES)
+        ]
+        u_codes = []
         u_scales = [keep.tile([P, J], U8, name=f"u_scales{z}", align_bytes=64) for z in range(PASSES)]
-        picked_scales = [keep.tile([P, I], U8, name=f"picked_scales{z}", align_bytes=64) for z in range(PASSES)]
-        wovens = [keep.tile([P, J * PACK], BF16, name=f"woven{z}", align_bytes=64) for z in range(PASSES)]
-        less = keep.tile([P, 2, 2, HALF], F32, name="less")
+        wovens = [keep.tile([P, J * PACK], BF16, name=f"woven{z}", tag=f"woven{z}", align_bytes=64) for z in range(PASSES)]
 
         def product(g):
             z, t = divmod(g, PACK)
-            picked = keep.tile([P, J], F32, name=f"picked{g}", tag=f"picked{g}")
+            picked = keep.tile([P, J], F32, name=f"picked{g}", tag=f"picked{g % 2}")
             window = xb_pairs[g // 2][:, (g % 2) * S : (g % 2 + 1) * S]
             nc.scalar.activation(picked[:], window.indirect(ent_list[:]), ACT.Copy)
-            scaled = keep.tile([P, J], F32, name=f"scaled{g}")
-            nc.scalar.activation(scaled[:], picked[:], ACT.Copy, scale=factors[:, z, t : t + 1])
-            pieces = 2 if g == planes - 1 else 1
-            width = J // pieces
-            for m in range(pieces):
+            scaled = keep.tile([P, J], F32, name=f"scaled{g}", tag=f"scaled{g}", align_bytes=64)
+            nc.scalar.activation(scaled[:], picked[:], ACT.Copy, scale=factors[:, t, z : z + 1])
+            width = J // pieces_of[z]
+            for m in range(pieces_of[z]):
                 cols = slice(m * width, (m + 1) * width)
                 nc.vector.tensor_tensor(
-                    prod[z][:, t, cols],
+                    prod[z][m][:, t, :],
                     xf_planes[g][:].indirect(tok_list[:, m * width // 16 : (m + 1) * width // 16]),
                     scaled[:, cols],
                     ALU.mult,
@@ -120,51 +121,64 @@ def tile_list_scores_products_listed_hinge_kernel(tc, xf, xb, fk, ky_words, ky_s
 
         def weave(z):
             woven = wovens[z]
-            copies = [nc.scalar.copy, nc.vector.tensor_copy] if z == PASSES - 1 else [nc.vector.tensor_copy]
-            width = J // len(copies)
-            for m, copy in enumerate(copies):
+            copy = nc.scalar.copy if z == PASSES - 1 else nc.vector.tensor_copy
+            width = J // pieces_of[z]
+            for m in range(pieces_of[z]):
                 dst = woven[:, m * width * PACK : (m + 1) * width * PACK].rearrange("p (c i t) -> p c t i", i=4, t=PACK)
-                src = prod[z][:, :, m * width : (m + 1) * width].rearrange("p t (c i) -> p c t i", i=4)
+                src = prod[z][m][:].rearrange("p t (c i) -> p c t i", i=4)
                 copy(dst, src)
 
-        def quantize(z):
+        def quantize(z, tag):
+            u_codes.append(keep.tile([P, J], U32, name=f"u_codes{z}", tag=tag, align_bytes=64))
             nc.vector.quantize_mx(out=u_codes[z][:].bitcast(E5M2X4), scales=u_scales[z][:], in_=wovens[z][:])
 
-        picked_words = {}
-
-        def pick_words(z):
-            for h in range(2):
-                picked_words[z, h] = keep.tile([P, HALF], U32, name=f"picked_words{z}_{h}", align_bytes=64)
+        def pick_words(z, tag):
+            picked_words = keep.tile([P, I], U32, name=f"picked_words{z}", tag=tag, align_bytes=64)
+            pieces = 2 if z == PASSES - 1 else 1
+            width = I // pieces
+            for h in range(pieces):
                 nc.vector.tensor_copy(
-                    picked_words[z, h][:],
-                    words[z][:].bitcast(U32).indirect(key_list[:, h * LIST_COLS : (h + 1) * LIST_COLS]),
+                    picked_words[:, h * width : (h + 1) * width],
+                    words[z][:].bitcast(U32).indirect(key_list[:, h * width // 16 : (h + 1) * width // 16]),
                 )
+            return picked_words
 
-        def pick_scales(z):
-            nc.vector.tensor_copy(picked_scales[z][:], key_scales[:, z * V : (z + 1) * V].indirect(key_list[:]))
-
-        def thresholds():
-            bias_rows = psum.tile([P, 2, HALF], F32, name="bias_rows")
-            for h in range(2):
-                nc.tensor.transpose(bias_rows[:, h, :], bias_cols[:, h : h + 1].to_broadcast([P, P]), ident[:])
-            for m in range(2):
-                nc.scalar.activation(
-                    less[:, :, m, :], bias_rows[:], ACT.Identity, bias=targets[:, m : m + 1], scale=-1.0
+        def pick_scales(tag):
+            picked_scales = keep.tile([P, PASSES * I], U8, name="picked_scales", tag=tag, align_bytes=64)
+            for z in range(PASSES):
+                nc.vector.tensor_copy(
+                    picked_scales[:, z * I : (z + 1) * I], key_scales[:, z * V : (z + 1) * V].indirect(key_list[:])
                 )
+            return picked_scales
 
-        for g in range(PACK):
+        turned_factors = psum.tile([P, PACK, P], F32, name="turned_factors")
+        for t in range(PACK):
+            nc.tensor.transpose(turned_factors[:, t, :], rows[:, t : P * PACK : PACK], ident[:])
+        nc.vector.tensor_copy(factors[:], turned_factors[:, :, 0:PASSES])
+        turned_rows = psum.tile([P, P], F32, name="turned_rows")
+        nc.tensor.transpose(turned_rows[:], rows[:, 0:P], ident[:])
+        nc.vector.tensor_copy(columns[:], turned_rows[:, 2:6])
+        bias_rows = psum.tile([P, 2, HALF], F32, name="bias_rows")
+        for h in range(2):
+            nc.tensor.transpose(bias_rows[:, h, :], columns[:, 2 + h : 3 + h].to_broadcast([P, P]), ident[:])
+        for m in range(2):
+            nc.vector.tensor_scalar(
+                out=shift[:, :, m, :], in0=bias_rows[:], scalar1=columns[:, m : m + 1], scalar2=None, op0=ALU.subtract
+            )
+
+        for g in range(3):
             product(g)
+        picked_scales = pick_scales("scaled2")
+        product(3)
         weave(0)
-        pick_scales(0)
-        quantize(0)
-        pick_scales(1)
-        for g in range(PACK, planes):
+        product(4)
+        quantize(0, "u_codes0")
+        for g in range(5, planes):
             product(g)
-        thresholds()
         weave(1)
-        pick_words(0)
-        quantize(1)
-        pick_words(1)
+        picked_words = [pick_words(0, "scaled7")]
+        quantize(1, "words0")
+        picked_words.append(pick_words(1, "woven1"))
 
         sums = [psum.tile([P, 2, HALF], F32, name=f"sums{h}") for h in range(2)]
         for z in range(PASSES):
@@ -174,8 +188,8 @@ def tile_list_scores_products_listed_hinge_kernel(tc, xf, xb, fk, ky_words, ky_s
                         out=sums[h][:, m, :],
                         lhsT=u_codes[z][:, m * HALF : (m + 1) * HALF].bitcast(E5M2X4),
                         lhsT_scale=u_scales[z][:, m * HALF : (m + 1) * HALF],
-                        rhs=picked_words[z, h][:].bitcast(E5M2X4),
-                        rhs_scale=picked_scales[z][:, h * HALF : (h + 1) * HALF],
+                        rhs=picked_words[z][:, h * HALF : (h + 1) * HALF].bitcast(E5M2X4),
+                        rhs_scale=picked_scales[:, z * I + h * HALF : z * I + (h + 1) * HALF],
                         start=(z == 0 and m == 0),
                         stop=(z == PASSES - 1 and m == 1),
                     )
@@ -186,8 +200,8 @@ def tile_list_scores_products_listed_hinge_kernel(tc, xf, xb, fk, ky_words, ky_s
             nc.vector.tensor_tensor(
                 margin[h][:],
                 sums[h][:].rearrange("p m n -> p (m n)"),
-                less[:, h].rearrange("p m n -> p (m n)"),
-                ALU.subtract,
+                shift[:, h].rearrange("p m n -> p (m n)"),
+                ALU.add,
             )
         for h in range(2):
             result = keep.tile([P, 2 * HALF], F32, name=f"result{h}")

@@ -33,36 +33,30 @@ def tile_list_scores_products_listed_hinge_kernel(tc, xf, xb, fk, ky_words, ky_s
         ent_list = keep.tile([P, J // 16], U16, name="ent_list")
         key_list = keep.tile([P, I // 16], U16, name="key_list")
         xf_planes = [keep.tile([P, T], F32, name=f"xf{g}") for g in range(planes)]
-        xb_pairs = [keep.tile([P, 2 * S], F32, name=f"xb{u}") for u in range(planes // 2)]
+        xb_pass = [keep.tile([P, PACK * S], F32, name=f"xb{z}") for z in range(PASSES)]
         words = [keep.tile([P, V], I32, name=f"words{z}", tag=f"words{z}", align_bytes=64) for z in range(PASSES)]
         key_scales = keep.tile([P, PASSES * V], U8, name="key_scales")
         rows = keep.tile([P, P * PACK], F32, name="rows")
         factors = keep.tile([P, PACK, PASSES], F32, name="factors")
-        columns = keep.tile([P, 4], F32, name="columns")
-        shift = keep.tile([P, 2, 2, HALF], F32, name="shift")
+        short_rows = keep.tile([P, P], F32, name="short_rows")
         ident = keep.tile([P, P], F32, name="ident")
 
         xf_view = xf.rearrange("(z p t) c -> z t p c", z=PASSES, t=PACK)
-        xb_view = xb.rearrange("(z p u e) c -> z u p (e c)", z=PASSES, u=2, e=2)
+        xb_view = xb.rearrange("(z p t) c -> z p (t c)", z=PASSES, t=PACK)
         scale_rows = ky_scales.bitcast(I32)
 
         def load_xf(g):
             nc.sync.dma_start(out=xf_planes[g][:], in_=xf_view[g // PACK, g % PACK])
 
-        def load_xb(u):
-            nc.sync.dma_start(out=xb_pairs[u][:], in_=xb_view[u // 2, u % 2])
+        def load_xb(z):
+            nc.sync.dma_start(out=xb_pass[z][:], in_=xb_view[z])
 
         def load_words(z):
             nc.sync.dma_start(out=words[z][:], in_=ky_words[z].rearrange("p c r -> p (c r)").bitcast(I32))
 
-        def load_scales(q):
-            nc.sync.dma_start(
-                out=key_scales[32 * q : 32 * q + 4, :].bitcast(I32).rearrange("p (z c) -> p z c", z=PASSES),
-                in_=scale_rows[:, 4 * q : 4 * q + 4, :].rearrange("z r c -> r z c"),
-            )
-
         nc.vector.memset(rows[:], 0.0)
         nc.vector.memset(key_scales[:].bitcast(I32), 0)
+        nc.vector.memset(short_rows[:], 0.0)
         distance = keep.tile([P, P], F32, name="distance", tag="picked0")
         nc.gpsimd.iota(
             distance[:], pattern=[[1, P]], base=0, channel_multiplier=-1, allow_small_or_imprecise_dtypes=True
@@ -72,22 +66,20 @@ def tile_list_scores_products_listed_hinge_kernel(tc, xf, xb, fk, ky_words, ky_s
         nc.scalar.activation(ident[:], magnitude[:], ACT.Relu, bias=1.0, scale=-1.0)
         load_xb(0)
         nc.sync.dma_start(out=rows[0:2, :], in_=fk.rearrange("(z k) o -> z (k o)", z=PASSES))
-        nc.sync.dma_start(out=rows[2:4, 0:HALF], in_=tg.rearrange("(m p) o -> m (p o)", m=2))
-        nc.sync.dma_start(out=rows[4:6, 0:HALF], in_=bi.rearrange("o (h n) -> (o h) n", h=2))
         nc.sync.dma_start(ent_list[:], offs2)
+        nc.sync.dma_start(key_list[:], offs3)
+        nc.sync.dma_start(
+            out=key_scales[0:P:8, :].bitcast(I32).rearrange("q (z c) -> q z c", z=PASSES),
+            in_=scale_rows.rearrange("z q c -> q z c"),
+        )
         nc.sync.dma_start(tok_list[:], offs)
         load_xf(0)
-        load_xb(1)
-        nc.sync.dma_start(key_list[:], offs3)
         load_xf(1)
-        load_scales(0)
-        load_xb(2)
-        load_scales(1)
-        load_scales(2)
+        nc.sync.dma_start(out=short_rows[0:2, :], in_=tg.rearrange("(m p) o -> m (p o)", m=2))
+        nc.sync.dma_start(out=short_rows[2:4, :], in_=bi.rearrange("o (h n) -> (o h) n", h=2))
         load_xf(2)
-        load_scales(3)
-        load_xb(3)
         load_xf(3)
+        load_xb(1)
         for g in range(4, planes):
             load_xf(g)
         for z in range(PASSES):
@@ -105,7 +97,7 @@ def tile_list_scores_products_listed_hinge_kernel(tc, xf, xb, fk, ky_words, ky_s
         def product(g):
             z, t = divmod(g, PACK)
             picked = keep.tile([P, J], F32, name=f"picked{g}", tag=f"picked{g % 2}")
-            window = xb_pairs[g // 2][:, (g % 2) * S : (g % 2 + 1) * S]
+            window = xb_pass[z][:, t * S : (t + 1) * S]
             nc.scalar.activation(picked[:], window.indirect(ent_list[:]), ACT.Copy)
             scaled = keep.tile([P, J], F32, name=f"scaled{g}", tag=f"scaled{g}", align_bytes=64)
             nc.scalar.activation(scaled[:], picked[:], ACT.Copy, scale=factors[:, t, z : z + 1])
@@ -149,31 +141,40 @@ def tile_list_scores_products_listed_hinge_kernel(tc, xf, xb, fk, ky_words, ky_s
                 nc.vector.tensor_copy(
                     picked_scales[:, z * I : (z + 1) * I], key_scales[:, z * V : (z + 1) * V].indirect(key_list[:])
                 )
-            return picked_scales
+            placed = keep.tile([P, PASSES * I], U8, name="placed_scales", align_bytes=64)
+            nc.vector.tensor_copy(placed[:].bitcast(I32), picked_scales[:].bitcast(I32))
+            for r in range(1, 4):
+                nc.gpsimd.dma_start(out=placed[r:P:32, :].bitcast(I32), in_=picked_scales[8 * r : P : 32, :].bitcast(I32))
+            return placed
 
         turned_factors = psum.tile([P, PACK, P], F32, name="turned_factors")
         for t in range(PACK):
             nc.tensor.transpose(turned_factors[:, t, :], rows[:, t : P * PACK : PACK], ident[:])
         nc.vector.tensor_copy(factors[:], turned_factors[:, :, 0:PASSES])
-        turned_rows = psum.tile([P, P], F32, name="turned_rows")
-        nc.tensor.transpose(turned_rows[:], rows[:, 0:P], ident[:])
-        nc.vector.tensor_copy(columns[:], turned_rows[:, 2:6])
-        bias_rows = psum.tile([P, 2, HALF], F32, name="bias_rows")
-        for h in range(2):
-            nc.tensor.transpose(bias_rows[:, h, :], columns[:, 2 + h : 3 + h].to_broadcast([P, P]), ident[:])
-        for m in range(2):
-            nc.vector.tensor_scalar(
-                out=shift[:, :, m, :], in0=bias_rows[:], scalar1=columns[:, m : m + 1], scalar2=None, op0=ALU.subtract
-            )
 
+        def shifts():
+            turned_rows = psum.tile([P, P], F32, name="turned_rows")
+            nc.tensor.transpose(turned_rows[:], short_rows[:], ident[:])
+            columns = keep.tile([P, 4], F32, name="columns", tag="scaled1", align_bytes=64)
+            nc.vector.tensor_copy(columns[:], turned_rows[:, 0:4])
+            bias_rows = psum.tile([P, 2, HALF], F32, name="bias_rows")
+            for h in range(2):
+                nc.tensor.transpose(bias_rows[:, h, :], columns[:, 2 + h : 3 + h].to_broadcast([P, P]), ident[:])
+            shift = keep.tile([P, 2, 2, HALF], F32, name="shift", tag="scaled2", align_bytes=64)
+            for m in range(2):
+                nc.vector.tensor_scalar(
+                    out=shift[:, :, m, :], in0=bias_rows[:], scalar1=columns[:, m : m + 1], scalar2=None, op0=ALU.subtract
+                )
+            return shift
+
+        picked_scales = pick_scales("picked_scales")
         for g in range(3):
             product(g)
-        picked_scales = pick_scales("scaled2")
+        shift = shifts()
         product(3)
         weave(0)
-        product(4)
         quantize(0, "u_codes0")
-        for g in range(5, planes):
+        for g in range(PACK, planes):
             product(g)
         weave(1)
         picked_words = [pick_words(0, "scaled7")]

from contextlib import ExitStack

import concourse.mybir as mybir

K, T, J, I, S, V = 1024, 1024, 256, 256, 512, 1024
FLOPS = 2 * K * J * I

F32 = mybir.dt.float32
BF16 = mybir.dt.bfloat16
I32 = mybir.dt.int32
U32 = mybir.dt.uint32
U16 = mybir.dt.uint16
U8 = mybir.dt.uint8
E5M2X4 = mybir.dt.float8_e5m2_x4
ALU = mybir.AluOpType
ACT = mybir.ActivationFunctionType

P = 128
PACK = 4
PASSES = K // (P * PACK)
HALF = 128
LIST_COLS = HALF // 16


def tile_list_scores_products_listed_hinge_kernel(tc, xf, xb, fk, ky_words, ky_scales, bi, tg, offs, offs2, offs3, out):
    nc = tc.nc
    with ExitStack() as ctx:
        keep = ctx.enter_context(tc.tile_pool(name="keep", bufs=1))
        psum = ctx.enter_context(tc.psum_pool(name="psum", bufs=1))

        planes = PASSES * PACK
        tok_list = keep.tile([P, J // 16], U16, name="tok_list")
        ent_list = keep.tile([P, J // 16], U16, name="ent_list")
        key_list = keep.tile([P, I // 16], U16, name="key_list")
        xf_planes = [keep.tile([P, T], F32, name=f"xf{g}") for g in range(planes)]
        xb_pass = [keep.tile([P, PACK * S], F32, name=f"xb{z}") for z in range(PASSES)]
        words = [keep.tile([P, V], I32, name=f"words{z}", tag=f"words{z}", align_bytes=64) for z in range(PASSES)]
        key_scales = keep.tile([P, PASSES * V], U8, name="key_scales")
        rows = keep.tile([P, P * PACK], F32, name="rows")
        factors = keep.tile([P, PACK, PASSES], F32, name="factors")
        short_rows = keep.tile([P, P], F32, name="short_rows")
        ident = keep.tile([P, P], F32, name="ident")

        xf_view = xf.rearrange("(z p t) c -> z t p c", z=PASSES, t=PACK)
        xb_view = xb.rearrange("(z p t) c -> z p (t c)", z=PASSES, t=PACK)
        scale_rows = ky_scales.bitcast(I32)

        def load_xf(g):
            nc.sync.dma_start(out=xf_planes[g][:], in_=xf_view[g // PACK, g % PACK])

        def load_xb(z):
            nc.sync.dma_start(out=xb_pass[z][:], in_=xb_view[z])

        def load_words(z):
            nc.sync.dma_start(out=words[z][:], in_=ky_words[z].rearrange("p c r -> p (c r)").bitcast(I32))

        nc.vector.memset(rows[:], 0.0)
        nc.vector.memset(key_scales[:].bitcast(I32), 0)
        nc.vector.memset(short_rows[:], 0.0)
        distance = keep.tile([P, P], F32, name="distance", tag="picked0")
        nc.gpsimd.iota(
            distance[:], pattern=[[1, P]], base=0, channel_multiplier=-1, allow_small_or_imprecise_dtypes=True
        )
        magnitude = keep.tile([P, P], F32, name="magnitude", tag="picked1")
        nc.scalar.activation(magnitude[:], distance[:], ACT.Abs)
        nc.scalar.activation(ident[:], magnitude[:], ACT.Relu, bias=1.0, scale=-1.0)
        load_xb(0)
        nc.sync.dma_start(out=rows[0:2, :], in_=fk.rearrange("(z k) o -> z (k o)", z=PASSES))
        nc.sync.dma_start(ent_list[:], offs2)
        nc.sync.dma_start(key_list[:], offs3)
        nc.sync.dma_start(
            out=key_scales[0:P:8, :].bitcast(I32).rearrange("q (z c) -> q z c", z=PASSES),
            in_=scale_rows.rearrange("z q c -> q z c"),
        )
        nc.sync.dma_start(tok_list[:], offs)
        load_xf(0)
        load_xf(1)
        nc.sync.dma_start(out=short_rows[0:2, :], in_=tg.rearrange("(m p) o -> m (p o)", m=2))
        nc.sync.dma_start(out=short_rows[2:4, :], in_=bi.rearrange("o (h n) -> (o h) n", h=2))
        load_xf(2)
        load_xf(3)
        load_xb(1)
        for g in range(4, planes):
            load_xf(g)
        for z in range(PASSES):
            load_words(z)

        pieces_of = [1, 2]
        prod = [
            [keep.tile([P, PACK, J // pieces_of[z]], F32, name=f"prod{z}_{m}") for m in range(pieces_of[z])]
            for z in range(PASSES)
        ]
        u_codes = []
        u_scales = [keep.tile([P, J], U8, name=f"u_scales{z}", align_bytes=64) for z in range(PASSES)]
        wovens = [keep.tile([P, J * PACK], BF16, name=f"woven{z}", tag=f"woven{z}", align_bytes=64) for z in range(PASSES)]

        def product(g):
            z, t = divmod(g, PACK)
            picked = keep.tile([P, J], F32, name=f"picked{g}", tag=f"picked{g % 2}")
            window = xb_pass[z][:, t * S : (t + 1) * S]
            nc.scalar.activation(picked[:], window.indirect(ent_list[:]), ACT.Copy)
            scaled = keep.tile([P, J], F32, name=f"scaled{g}", tag=f"scaled{g}", align_bytes=64)
            nc.scalar.activation(scaled[:], picked[:], ACT.Copy, scale=factors[:, t, z : z + 1])
            width = J // pieces_of[z]
            for m in range(pieces_of[z]):
                cols = slice(m * width, (m + 1) * width)
                nc.vector.tensor_tensor(
                    prod[z][m][:, t, :],
                    xf_planes[g][:].indirect(tok_list[:, m * width // 16 : (m + 1) * width // 16]),
                    scaled[:, cols],
                    ALU.mult,
                )

        def weave(z):
            woven = wovens[z]
            copy = nc.scalar.copy if z == PASSES - 1 else nc.vector.tensor_copy
            width = J // pieces_of[z]
            for m in range(pieces_of[z]):
                dst = woven[:, m * width * PACK : (m + 1) * width * PACK].rearrange("p (c i t) -> p c t i", i=4, t=PACK)
                src = prod[z][m][:].rearrange("p t (c i) -> p c t i", i=4)
                copy(dst, src)

        def quantize(z, tag):
            u_codes.append(keep.tile([P, J], U32, name=f"u_codes{z}", tag=tag, align_bytes=64))
            nc.vector.quantize_mx(out=u_codes[z][:].bitcast(E5M2X4), scales=u_scales[z][:], in_=wovens[z][:])

        def pick_words(z, tag):
            picked_words = keep.tile([P, I], U32, name=f"picked_words{z}", tag=tag, align_bytes=64)
            pieces = 2 if z == PASSES - 1 else 1
            width = I // pieces
            for h in range(pieces):
                nc.vector.tensor_copy(
                    picked_words[:, h * width : (h + 1) * width],
                    words[z][:].bitcast(U32).indirect(key_list[:, h * width // 16 : (h + 1) * width // 16]),
                )
            return picked_words

        def pick_scales(tag):
            picked_scales = keep.tile([P, PASSES * I], U8, name="picked_scales", tag=tag, align_bytes=64)
            for z in range(PASSES):
                nc.vector.tensor_copy(
                    picked_scales[:, z * I : (z + 1) * I], key_scales[:, z * V : (z + 1) * V].indirect(key_list[:])
                )
            placed = keep.tile([P, PASSES * I], U8, name="placed_scales", align_bytes=64)
            nc.vector.tensor_copy(placed[:].bitcast(I32), picked_scales[:].bitcast(I32))
            for r in range(1, 4):
                nc.gpsimd.dma_start(out=placed[r:P:32, :].bitcast(I32), in_=picked_scales[8 * r : P : 32, :].bitcast(I32))
            return placed

        turned_factors = psum.tile([P, PACK, P], F32, name="turned_factors")
        for t in range(PACK):
            nc.tensor.transpose(turned_factors[:, t, :], rows[:, t : P * PACK : PACK], ident[:])
        nc.vector.tensor_copy(factors[:], turned_factors[:, :, 0:PASSES])

        def shifts():
            turned_rows = psum.tile([P, P], F32, name="turned_rows")
            nc.tensor.transpose(turned_rows[:], short_rows[:], ident[:])
            columns = keep.tile([P, 4], F32, name="columns", tag="scaled1", align_bytes=64)
            nc.vector.tensor_copy(columns[:], turned_rows[:, 0:4])
            bias_rows = psum.tile([P, 2, HALF], F32, name="bias_rows")
            for h in range(2):
                nc.tensor.transpose(bias_rows[:, h, :], columns[:, 2 + h : 3 + h].to_broadcast([P, P]), ident[:])
            shift = keep.tile([P, 2, 2, HALF], F32, name="shift", tag="scaled2", align_bytes=64)
            for m in range(2):
                nc.vector.tensor_scalar(
                    out=shift[:, :, m, :], in0=bias_rows[:], scalar1=columns[:, m : m + 1], scalar2=None, op0=ALU.subtract
                )
            return shift

        picked_scales = pick_scales("picked_scales")
        for g in range(3):
            product(g)
        shift = shifts()
        product(3)
        weave(0)
        quantize(0, "u_codes0")
        for g in range(PACK, planes):
            product(g)
        weave(1)
        picked_words = [pick_words(0, "scaled7")]
        quantize(1, "words0")
        picked_words.append(pick_words(1, "woven1"))

        sums = [psum.tile([P, 2, HALF], F32, name=f"sums{h}") for h in range(2)]
        for z in range(PASSES):
            for h in range(2):
                for m in range(2):
                    nc.tensor.matmul_mx(
                        out=sums[h][:, m, :],
                        lhsT=u_codes[z][:, m * HALF : (m + 1) * HALF].bitcast(E5M2X4),
                        lhsT_scale=u_scales[z][:, m * HALF : (m + 1) * HALF],
                        rhs=picked_words[z][:, h * HALF : (h + 1) * HALF].bitcast(E5M2X4),
                        rhs_scale=picked_scales[:, z * I + h * HALF : z * I + (h + 1) * HALF],
                        start=(z == 0 and m == 0),
                        stop=(z == PASSES - 1 and m == 1),
                    )

        out_view = out.rearrange("(m p) (h n) -> h p m n", m=2, h=2)
        margin = [keep.tile([P, 2 * HALF], F32, name=f"margin{h}") for h in range(2)]
        for h in range(2):
            nc.vector.tensor_tensor(
                margin[h][:],
                sums[h][:].rearrange("p m n -> p (m n)"),
                shift[:, h].rearrange("p m n -> p (m n)"),
                ALU.add,
            )
        for h in range(2):
            result = keep.tile([P, 2 * HALF], F32, name=f"result{h}")
            if h == 0:
                excess = keep.tile([P, 2 * HALF], F32, name="excess")
                nc.scalar.activation(excess[:], margin[h][:], ACT.Relu)
                nc.scalar.activation(result[:], excess[:], ACT.Square)
            else:
                nc.vector.scalar_tensor_tensor(result[:], margin[h][:], 0.0, margin[h][:], ALU.max, ALU.mult)
            queue = nc.scalar if h == 0 else nc.sync
            queue.dma_start(out=out_view[h], in_=result[:].rearrange("p (m n) -> p m n", m=2))
